import numpy as np
import ml_dtypes


def mxq(x, axis, fmt="e4m3"):
    dtype, down = {"e4m3": (ml_dtypes.float8_e4m3fn, 7), "e5m2": (ml_dtypes.float8_e5m2, 14)}[fmt]
    v = np.moveaxis(np.asarray(x, np.float32).astype(ml_dtypes.bfloat16).astype(np.float64), axis, -1)
    blocks = v.reshape(v.shape[:-1] + (-1, 32))
    amax = np.abs(blocks).max(-1, keepdims=True)
    byte = np.maximum(np.where(amax > 0, np.frexp(amax)[1] - 1 + 127, 0) - down, 1)
    scale = np.exp2(byte - 127.0)
    codes = (blocks / scale).astype(np.float32).astype(dtype).astype(np.float64)
    return np.moveaxis((codes * scale).reshape(v.shape), -1, axis)


WIDE = False


def mx_kscale(k):
    if not WIDE:
        return np.ones(k)
    levels = np.array([10, -10, 5, -5, 0])
    if k % 512:
        return np.exp2(np.random.permutation(np.resize(levels, k // 32))).repeat(32)
    a = np.empty((k // 512, 16))
    for p in range(k // 512):
        a[p, :8] = np.random.permutation(np.resize(levels, 8))
        for g in range(8):
            far = levels[np.abs(levels - a[p, g]) >= 10]
            a[p, g + 8] = far[np.random.randint(len(far))]
    return np.exp2(a.ravel()).repeat(32)


def f64(x):
    return np.asarray(x).astype(np.float64)


def striped(idx):
    return np.tile(idx.reshape(-1, 16).T, (8, 1)).astype(np.uint16)


def unstriped(offs):
    return offs[:16].T.reshape(-1).astype(np.int64)


def gelu(v):
    return 0.5 * v * (1.0 + np.tanh(np.sqrt(2.0 / np.pi) * (v + 0.044715 * v**3)))


K, T, D, S, V, N = 512, 2048, 3, 1024, 512, 256


def setup_inputs():
    n = np.random.standard_normal
    s = mx_kscale(K)[:, None]
    return {
        "xT": (n((K, T)) * s).astype(np.float32),
        "w": (n((K, N)) / np.sqrt(K) / s).astype(np.float32),
        "b": (0.3 * n((N, 1))).astype(np.float32),
        "gate": np.tile(np.random.uniform(0.2, 1.0, (D, 1, V)) / np.sqrt(D), (1, N, 1)).astype(np.float32),
        "offs": striped(np.random.permutation(T)[:S]),
        "pos1": striped(np.random.permutation(S)[:V]),
        "pos2": striped(np.random.permutation(S)[:V]),
        "pos3": striped(np.random.permutation(S)[:V]),
    }


def reference(xT, w, b, gate, offs, pos1, pos2, pos3):
    idx = unstriped(offs)
    xq = mxq(f64(xT)[:, idx], 0, "e4m3")
    y = mxq(f64(w), 0, "e4m3").T @ xq
    y = gelu(y + f64(b))
    return sum(f64(gate[d]) * y[:, unstriped(p)] for d, p in enumerate((pos1, pos2, pos3)))

@@ -1,0 +1,172 @@
+from contextlib import ExitStack
+
+import concourse.mybir as mybir
+
+K, T, D, S, V, N = 512, 2048, 3, 1024, 512, 256
+P = 128
+
+F32 = mybir.dt.float32
+BF16 = mybir.dt.bfloat16
+U32 = mybir.dt.uint32
+U16 = mybir.dt.uint16
+U8 = mybir.dt.uint8
+FP8X4 = mybir.dt.float8_e4m3fn_x4
+
+ACT = mybir.ActivationFunctionType
+ALU = mybir.AluOpType
+
+FLOPS = 2 * K * S * N
+
+CHUNKS = (
+    ((1024, 400), (512, 200), (512, 200)),
+    ((512, 384), (512, 384), (512, 320), (256, 96), (256, 96)),
+)
+SLICES = ((0, 512), (512, 768), (768, 1024))
+
+
+def tile_picked_sub_lin_gelu_sub_e_kernel(tc, xT, w, b, gate, offs, pos1, pos2, pos3, out):
+    nc = tc.nc
+    x_view = xT.rearrange("(p u j) t -> p u j t", u=2, j=2)
+    gate_view = gate.rearrange("d (p m) v -> d p (m v)", m=2)
+    out_view = out.rearrange("(p m) v -> p m v", m=2)
+
+    with ExitStack() as ctx:
+        lists = ctx.enter_context(tc.tile_pool(name="lists", bufs=1))
+        keep = ctx.enter_context(tc.tile_pool(name="keep", bufs=1))
+        psum = ctx.enter_context(tc.psum_pool(name="psum", bufs=1))
+
+        offs_sb = lists.tile([P, S // 16], U16, name="offs_sb")
+        pos_sb = [lists.tile([P, V // 16], U16, name=f"pos_sb{d}") for d in range(D)]
+
+        zero = keep.tile([P, 1], F32, name="zero")
+        nc.vector.memset(zero[:], 0.0)
+        warm = keep.tile([P, 1], F32, name="warm")
+        nc.scalar.activation(warm[:], zero[:], ACT.Gelu_apprx_tanh)
+
+        nc.sync.dma_start(offs_sb[:], offs)
+        raw = []
+        for u in range(2):
+            c0 = 0
+            for i, (width, act_cols) in enumerate(CHUNKS[u]):
+                r = keep.tile([P, 2, width], F32, name=f"raw{u}_{i}")
+                nc.sync.dma_start(out=r[:], in_=x_view[:, u, :, c0 : c0 + width])
+                raw.append((u, c0, width, act_cols, r))
+                c0 += width
+        w_raw = keep.tile([P, 4, N], F32, name="w_raw")
+        nc.sync.dma_start(out=w_raw[:], in_=w.rearrange("(p j) c -> p j c", j=4))
+        bias = keep.tile([P, 2], F32, name="bias")
+        nc.sync.dma_start(out=bias[:], in_=b.rearrange("(p m) o -> p (m o)", m=2))
+        gates = []
+        for d, p_in in enumerate((pos1, pos2, pos3)):
+            nc.sync.dma_start(pos_sb[d][:], p_in)
+            g = keep.tile([P, 2, V], F32, name=f"gate{d}")
+            nc.sync.dma_start(out=g[:].rearrange("p m v -> p (m v)"), in_=gate_view[d])
+            gates.append(g)
+
+        pair = [keep.tile([P, T, 2], BF16, name=f"pair{u}", align_bytes=64) for u in range(2)]
+        grouped = keep.tile([P, S, 4], BF16, name="grouped", align_bytes=64)
+        grouped_words = grouped[:].rearrange("p s j -> p (s j)").bitcast(U32).rearrange("p (s u) -> p u s", u=2)
+
+        def cast(u):
+            for uu, c0, width, act_cols, r in raw:
+                if uu != u:
+                    continue
+                src = r[:].rearrange("p j t -> p t j")
+                vec = width - act_cols
+                nc.scalar.activation(pair[u][:, c0 + vec : c0 + width, :], src[:, vec:, :], ACT.Copy)
+                nc.vector.tensor_copy(out=pair[u][:, c0 : c0 + vec, :], in_=src[:, :vec, :])
+
+        def gather(u, a, e):
+            window = pair[u][:].rearrange("p t j -> p (t j)").bitcast(U32)
+            nc.vector.tensor_copy(
+                out=grouped_words[:, u, a:e], in_=window.indirect(offs_sb[:, a // 16 : e // 16])
+            )
+
+        x_codes = [keep.tile([P, e - a], U32, name=f"x_codes{i}", align_bytes=64) for i, (a, e) in enumerate(SLICES)]
+        x_scales = [keep.tile([P, e - a], U8, name=f"x_scales{i}", align_bytes=64) for i, (a, e) in enumerate(SLICES)]
+
+        def quantize(i):
+            a, e = SLICES[i]
+            nc.vector.quantize_mx(
+                out=x_codes[i][:].bitcast(FP8X4),
+                scales=x_scales[i][:],
+                in_=grouped[:, a:e, :].rearrange("p s j -> p (s j)"),
+            )
+
+        cast(0)
+        gather(0, 0, S)
+        cast(1)
+
+        w_grouped = keep.tile([P, N, 4], BF16, name="w_grouped", align_bytes=64)
+        nc.scalar.activation(
+            w_grouped[:].rearrange("p (m c) j -> p m c j", m=2),
+            w_raw[:].rearrange("p j (c m) -> p m c j", m=2),
+            ACT.Copy,
+        )
+        w_codes = keep.tile([P, N], U32, name="w_codes", align_bytes=64)
+        w_scales = keep.tile([P, N], U8, name="w_scales", align_bytes=64)
+
+        gather(1, *SLICES[0])
+        gather(1, *SLICES[1])
+        quantize(0)
+        nc.vector.quantize_mx(
+            out=w_codes[:].bitcast(FP8X4),
+            scales=w_scales[:],
+            in_=w_grouped[:].rearrange("p n j -> p (n j)"),
+        )
+        gather(1, *SLICES[2])
+        quantize(1)
+        quantize(2)
+
+        acc = {}
+        for i, (a, e) in enumerate(SLICES):
+            for m in range(2):
+                bank = psum.tile([P, e - a], F32, name=f"acc{i}_{m}")
+                cols = slice(m * P, (m + 1) * P)
+                nc.tensor.matmul_mx(
+                    out=bank[:],
+                    lhsT=w_codes[:, cols].bitcast(FP8X4),
+                    lhsT_scale=w_scales[:, cols],
+                    rhs=x_codes[i][:].bitcast(FP8X4),
+                    rhs_scale=x_scales[i][:],
+                    start=True,
+                    stop=True,
+                )
+                acc[i, m] = bank
+
+        y = [keep.tile([P, S], F32, name=f"y{m}") for m in range(2)]
+        for i, m in ((0, 0), (0, 1), (1, 0), (2, 0), (1, 1), (2, 1)):
+            a, e = SLICES[i]
+            nc.scalar.activation(y[m][:, a:e], acc[i, m][:], ACT.Gelu_apprx_tanh, bias=bias[:, m : m + 1])
+
+        prod = [[keep.tile([P, V], F32, name=f"prod{m}_{d}") for d in range(D)] for m in range(2)]
+        part = [keep.tile([P, V], F32, name=f"part{m}") for m in range(2)]
+        res = [keep.tile([P, V], F32, name=f"res{m}") for m in range(2)]
+
+        def neighbour(m, d, a=0, e=V):
+            nc.vector.tensor_tensor(
+                prod[m][d][:, a:e],
+                y[m][:].indirect(pos_sb[d][:, a // 16 : e // 16]),
+                gates[d][:, m, a:e],
+                ALU.mult,
+            )
+
+        def first_sum(m):
+            nc.vector.tensor_tensor(part[m][:], prod[m][0][:], prod[m][1][:], ALU.add)
+
+        def last_sum(m, a=0, e=V):
+            nc.vector.tensor_tensor(res[m][:, a:e], part[m][:, a:e], prod[m][2][:, a:e], ALU.add)
+            nc.sync.dma_start(out=out_view[:, m, a:e], in_=res[m][:, a:e])
+
+        neighbour(0, 0)
+        neighbour(0, 1)
+        neighbour(1, 0)
+        first_sum(0)
+        neighbour(0, 2)
+        neighbour(1, 1)
+        last_sum(0)
+        first_sum(1)
+        neighbour(1, 2, 0, 256)
+        neighbour(1, 2, 256, V)
+        last_sum(1, 0, 256)
+        last_sum(1, 256, V)

@@ -18,10 +18,10 @@ ALU = mybir.AluOpType
 FLOPS = 2 * K * S * N
 
 CHUNKS = (
-    ((1024, 400), (512, 200), (512, 200)),
-    ((512, 384), (512, 384), (512, 320), (256, 96), (256, 96)),
+    ((512, 160), (512, 160), (512, 160), (256, 64), (256, 64)),
+    ((512, 512), (512, 448), (512, 320), (256, 128), (256, 64)),
 )
-SLICES = ((0, 512), (512, 768), (768, 1024))
+STEP = 256
 
 
 def tile_picked_sub_lin_gelu_sub_e_kernel(tc, xT, w, b, gate, offs, pos1, pos2, pos3, out):
@@ -43,7 +43,6 @@ def tile_picked_sub_lin_gelu_sub_e_kernel(tc, xT, w, b, gate, offs, pos1, pos2, 
         warm = keep.tile([P, 1], F32, name="warm")
         nc.scalar.activation(warm[:], zero[:], ACT.Gelu_apprx_tanh)
 
-        nc.sync.dma_start(offs_sb[:], offs)
         raw = []
         for u in range(2):
             c0 = 0
@@ -52,6 +51,8 @@ def tile_picked_sub_lin_gelu_sub_e_kernel(tc, xT, w, b, gate, offs, pos1, pos2, 
                 nc.sync.dma_start(out=r[:], in_=x_view[:, u, :, c0 : c0 + width])
                 raw.append((u, c0, width, act_cols, r))
                 c0 += width
+                if len(raw) == 2:
+                    nc.sync.dma_start(offs_sb[:], offs)
         w_raw = keep.tile([P, 4, N], F32, name="w_raw")
         nc.sync.dma_start(out=w_raw[:], in_=w.rearrange("(p j) c -> p j c", j=4))
         bias = keep.tile([P, 2], F32, name="bias")
@@ -73,8 +74,10 @@ def tile_picked_sub_lin_gelu_sub_e_kernel(tc, xT, w, b, gate, offs, pos1, pos2, 
                     continue
                 src = r[:].rearrange("p j t -> p t j")
                 vec = width - act_cols
-                nc.scalar.activation(pair[u][:, c0 + vec : c0 + width, :], src[:, vec:, :], ACT.Copy)
-                nc.vector.tensor_copy(out=pair[u][:, c0 : c0 + vec, :], in_=src[:, :vec, :])
+                if act_cols > 0:
+                    nc.scalar.activation(pair[u][:, c0 + vec : c0 + width, :], src[:, vec:, :], ACT.Copy)
+                if vec > 0:
+                    nc.vector.tensor_copy(out=pair[u][:, c0 : c0 + vec, :], in_=src[:, :vec, :])
 
         def gather(u, a, e):
             window = pair[u][:].rearrange("p t j -> p (t j)").bitcast(U32)
@@ -82,14 +85,13 @@ def tile_picked_sub_lin_gelu_sub_e_kernel(tc, xT, w, b, gate, offs, pos1, pos2, 
                 out=grouped_words[:, u, a:e], in_=window.indirect(offs_sb[:, a // 16 : e // 16])
             )
 
-        x_codes = [keep.tile([P, e - a], U32, name=f"x_codes{i}", align_bytes=64) for i, (a, e) in enumerate(SLICES)]
-        x_scales = [keep.tile([P, e - a], U8, name=f"x_scales{i}", align_bytes=64) for i, (a, e) in enumerate(SLICES)]
+        x_codes = keep.tile([P, S], U32, name="x_codes", align_bytes=64)
+        x_scales = keep.tile([P, S], U8, name="x_scales", align_bytes=64)
 
-        def quantize(i):
-            a, e = SLICES[i]
+        def quantize(a, e):
             nc.vector.quantize_mx(
-                out=x_codes[i][:].bitcast(FP8X4),
-                scales=x_scales[i][:],
+                out=x_codes[:, a:e].bitcast(FP8X4),
+                scales=x_scales[:, a:e],
                 in_=grouped[:, a:e, :].rearrange("p s j -> p (s j)"),
             )
 
@@ -97,76 +99,82 @@ def tile_picked_sub_lin_gelu_sub_e_kernel(tc, xT, w, b, gate, offs, pos1, pos2, 
         gather(0, 0, S)
         cast(1)
 
-        w_grouped = keep.tile([P, N, 4], BF16, name="w_grouped", align_bytes=64)
-        nc.scalar.activation(
-            w_grouped[:].rearrange("p (m c) j -> p m c j", m=2),
-            w_raw[:].rearrange("p j (c m) -> p m c j", m=2),
-            ACT.Copy,
-        )
-        w_codes = keep.tile([P, N], U32, name="w_codes", align_bytes=64)
-        w_scales = keep.tile([P, N], U8, name="w_scales", align_bytes=64)
+        w_grouped = [keep.tile([P, P, 4], BF16, name=f"w_grouped{m}", align_bytes=64) for m in range(2)]
+        w_codes = [keep.tile([P, P], U32, name=f"w_codes{m}", align_bytes=64) for m in range(2)]
+        w_scales = [keep.tile([P, P], U8, name=f"w_scales{m}", align_bytes=64) for m in range(2)]
+        for m in range(2):
+            nc.gpsimd.tensor_scalar(
+                out=w_grouped[m][:],
+                in0=w_raw[:].rearrange("p j (c m) -> p m c j", m=2)[:, m, :, :],
+                scalar1=1.0,
+                scalar2=0.0,
+                op0=ALU.mult,
+                op1=ALU.add,
+            )
 
-        gather(1, *SLICES[0])
-        gather(1, *SLICES[1])
-        quantize(0)
-        nc.vector.quantize_mx(
-            out=w_codes[:].bitcast(FP8X4),
-            scales=w_scales[:],
-            in_=w_grouped[:].rearrange("p n j -> p (n j)"),
-        )
-        gather(1, *SLICES[2])
-        quantize(1)
-        quantize(2)
+        def quantize_w(m):
+            nc.vector.quantize_mx(
+                out=w_codes[m][:].bitcast(FP8X4),
+                scales=w_scales[m][:],
+                in_=w_grouped[m][:].rearrange("p n j -> p (n j)"),
+            )
 
-        acc = {}
-        for i, (a, e) in enumerate(SLICES):
-            for m in range(2):
-                bank = psum.tile([P, e - a], F32, name=f"acc{i}_{m}")
-                cols = slice(m * P, (m + 1) * P)
-                nc.tensor.matmul_mx(
-                    out=bank[:],
-                    lhsT=w_codes[:, cols].bitcast(FP8X4),
-                    lhsT_scale=w_scales[:, cols],
-                    rhs=x_codes[i][:].bitcast(FP8X4),
-                    rhs_scale=x_scales[i][:],
-                    start=True,
-                    stop=True,
-                )
-                acc[i, m] = bank
+        gather(1, 0, 768)
+        gather(1, 768, S)
+        quantize_w(0)
+        for a in range(0, S, STEP):
+            quantize(a, a + STEP)
+        quantize_w(1)
 
         y = [keep.tile([P, S], F32, name=f"y{m}") for m in range(2)]
-        for i, m in ((0, 0), (0, 1), (1, 0), (2, 0), (1, 1), (2, 1)):
-            a, e = SLICES[i]
-            nc.scalar.activation(y[m][:, a:e], acc[i, m][:], ACT.Gelu_apprx_tanh, bias=bias[:, m : m + 1])
 
-        prod = [[keep.tile([P, V], F32, name=f"prod{m}_{d}") for d in range(D)] for m in range(2)]
-        part = [keep.tile([P, V], F32, name=f"part{m}") for m in range(2)]
-        res = [keep.tile([P, V], F32, name=f"res{m}") for m in range(2)]
+        def layer(m, a, e, tag):
+            bank = psum.tile([P, e - a], F32, name=f"acc{m}_{a}", tag=tag)
+            nc.tensor.matmul_mx(
+                out=bank[:],
+                lhsT=w_codes[m][:].bitcast(FP8X4),
+                lhsT_scale=w_scales[m][:],
+                rhs=x_codes[:, a:e].bitcast(FP8X4),
+                rhs_scale=x_scales[:, a:e],
+                start=True,
+                stop=True,
+            )
+            nc.scalar.activation(y[m][:, a:e], bank[:], ACT.Gelu_apprx_tanh, bias=bias[:, m : m + 1])
+
+        for i in range(4):
+            layer(0, i * STEP, (i + 1) * STEP, f"bank{i}")
+        for i in range(2):
+            layer(1, i * 512, (i + 1) * 512, f"bank{3 - i}")
+
+        prod = [keep.tile([P, 2, V], F32, name=f"prod{d}") for d in range(D)]
+        part = keep.tile([P, 2, V], F32, name="part")
+        res = keep.tile([P, 2, V], F32, name="res")
 
         def neighbour(m, d, a=0, e=V):
             nc.vector.tensor_tensor(
-                prod[m][d][:, a:e],
+                prod[d][:, m, a:e],
                 y[m][:].indirect(pos_sb[d][:, a // 16 : e // 16]),
                 gates[d][:, m, a:e],
                 ALU.mult,
             )
 
-        def first_sum(m):
-            nc.vector.tensor_tensor(part[m][:], prod[m][0][:], prod[m][1][:], ALU.add)
-
         def last_sum(m, a=0, e=V):
-            nc.vector.tensor_tensor(res[m][:, a:e], part[m][:, a:e], prod[m][2][:, a:e], ALU.add)
-            nc.sync.dma_start(out=out_view[:, m, a:e], in_=res[m][:, a:e])
+            nc.vector.tensor_tensor(res[:, m, a:e], part[:, m, a:e], prod[2][:, m, a:e], ALU.add)
+            nc.sync.dma_start(out=out_view[:, m, a:e], in_=res[:, m, a:e])
 
         neighbour(0, 0)
         neighbour(0, 1)
-        neighbour(1, 0)
-        first_sum(0)
         neighbour(0, 2)
+        neighbour(1, 0)
         neighbour(1, 1)
-        last_sum(0)
-        first_sum(1)
         neighbour(1, 2, 0, 256)
+        nc.vector.tensor_tensor(
+            part[:].rearrange("p m v -> p (m v)"),
+            prod[0][:].rearrange("p m v -> p (m v)"),
+            prod[1][:].rearrange("p m v -> p (m v)"),
+            ALU.add,
+        )
         neighbour(1, 2, 256, V)
+        last_sum(0)
         last_sum(1, 0, 256)
         last_sum(1, 256, V)

@@ -17,18 +17,17 @@ ALU = mybir.AluOpType
 
 FLOPS = 2 * K * S * N
 
-CHUNKS = (
-    ((512, 160), (512, 160), (512, 160), (256, 64), (256, 64)),
-    ((512, 512), (512, 448), (512, 320), (256, 128), (256, 64)),
-)
-STEP = 256
+PAIR_CHUNKS = (512, 512, 512, 256, 256)
+LAST_CHUNKS = ((1024, 384), (512, 256), (512, 512))
+V_TOKENS = 512
+SLICES = ((0, 256), (256, 512), (512, 768), (768, 896), (896, 1024))
 
 
 def tile_picked_sub_lin_gelu_sub_e_kernel(tc, xT, w, b, gate, offs, pos1, pos2, pos3, out):
     nc = tc.nc
-    x_view = xT.rearrange("(p u j) t -> p u j t", u=2, j=2)
-    gate_view = gate.rearrange("d (p m) v -> d p (m v)", m=2)
-    out_view = out.rearrange("(p m) v -> p m v", m=2)
+    x_view = xT.rearrange("(p j) t -> p j t", j=4)
+    gate_view = gate.rearrange("d (m p) v -> d p m v", m=2)
+    out_view = out.rearrange("(m p) v -> p m v", m=2)
 
     with ExitStack() as ctx:
         lists = ctx.enter_context(tc.tile_pool(name="lists", bufs=1))
@@ -43,47 +42,67 @@ def tile_picked_sub_lin_gelu_sub_e_kernel(tc, xT, w, b, gate, offs, pos1, pos2, 
         warm = keep.tile([P, 1], F32, name="warm")
         nc.scalar.activation(warm[:], zero[:], ACT.Gelu_apprx_tanh)
 
+        raw0 = keep.tile([P, T], F32, name="raw0")
+        raw1 = keep.tile([P, T], F32, name="raw1")
+        half = T // 2
+        nc.sync.dma_start(out=raw0[:, :half], in_=x_view[:, 0, :half])
+        nc.sync.dma_start(offs_sb[:], offs)
+        nc.sync.dma_start(out=raw0[:, half:], in_=x_view[:, 0, half:])
         raw = []
-        for u in range(2):
-            c0 = 0
-            for i, (width, act_cols) in enumerate(CHUNKS[u]):
-                r = keep.tile([P, 2, width], F32, name=f"raw{u}_{i}")
-                nc.sync.dma_start(out=r[:], in_=x_view[:, u, :, c0 : c0 + width])
-                raw.append((u, c0, width, act_cols, r))
-                c0 += width
-                if len(raw) == 2:
-                    nc.sync.dma_start(offs_sb[:], offs)
-        w_raw = keep.tile([P, 4, N], F32, name="w_raw")
-        nc.sync.dma_start(out=w_raw[:], in_=w.rearrange("(p j) c -> p j c", j=4))
+        c0 = 0
+        for i, width in enumerate(PAIR_CHUNKS):
+            r = keep.tile([P, 2, width], F32, name=f"raw23_{i}")
+            nc.sync.dma_start(out=r[:], in_=x_view[:, 2:4, c0 : c0 + width])
+            raw.append((c0, width, r))
+            c0 += width
+        w_view = w.rearrange("(p j) c -> p j c", j=4)
+        w_raw = [keep.tile([P, 4, P], F32, name=f"w_raw{m}") for m in range(2)]
+        c0 = 0
+        for width, act_cols in LAST_CHUNKS:
+            if c0 + width == T:
+                nc.sync.dma_start(out=w_raw[0][:], in_=w_view[:, :, :P])
+            nc.sync.dma_start(out=raw1[:, c0 : c0 + width], in_=x_view[:, 1, c0 : c0 + width])
+            c0 += width
+        nc.sync.dma_start(out=w_raw[1][:], in_=w_view[:, :, P:])
         bias = keep.tile([P, 2], F32, name="bias")
-        nc.sync.dma_start(out=bias[:], in_=b.rearrange("(p m) o -> p (m o)", m=2))
+        nc.sync.dma_start(out=bias[:], in_=b.rearrange("(m p) o -> p (m o)", m=2))
         gates = []
         for d, p_in in enumerate((pos1, pos2, pos3)):
             nc.sync.dma_start(pos_sb[d][:], p_in)
             g = keep.tile([P, 2, V], F32, name=f"gate{d}")
-            nc.sync.dma_start(out=g[:].rearrange("p m v -> p (m v)"), in_=gate_view[d])
+            nc.sync.dma_start(out=g[:], in_=gate_view[d])
             gates.append(g)
 
-        pair = [keep.tile([P, T, 2], BF16, name=f"pair{u}", align_bytes=64) for u in range(2)]
         grouped = keep.tile([P, S, 4], BF16, name="grouped", align_bytes=64)
-        grouped_words = grouped[:].rearrange("p s j -> p (s j)").bitcast(U32).rearrange("p (s u) -> p u s", u=2)
+        words = grouped[:].rearrange("p s j -> p (s j)").bitcast(U32).rearrange("p (s u) -> p u s", u=2)
+        v_offs = offs_sb[:, 0 : V_TOKENS // 16]
+        s_offs = offs_sb[:, V_TOKENS // 16 : S // 16]
 
-        def cast(u):
-            for uu, c0, width, act_cols, r in raw:
-                if uu != u:
-                    continue
-                src = r[:].rearrange("p j t -> p t j")
-                vec = width - act_cols
-                if act_cols > 0:
-                    nc.scalar.activation(pair[u][:, c0 + vec : c0 + width, :], src[:, vec:, :], ACT.Copy)
-                if vec > 0:
-                    nc.vector.tensor_copy(out=pair[u][:, c0 : c0 + vec, :], in_=src[:, :vec, :])
+        plane0 = keep.tile([P, T], BF16, name="plane0", align_bytes=64)
+        for a in (0, half):
+            nc.scalar.activation(plane0[:, a : a + half], raw0[:, a : a + half], ACT.Copy)
+        nc.vector.tensor_copy(out=grouped[:, :V_TOKENS, 0], in_=raw0[:].indirect(v_offs))
+        nc.scalar.activation(grouped[:, V_TOKENS:, 0], plane0[:].indirect(s_offs), ACT.Copy)
 
-        def gather(u, a, e):
-            window = pair[u][:].rearrange("p t j -> p (t j)").bitcast(U32)
-            nc.vector.tensor_copy(
-                out=grouped_words[:, u, a:e], in_=window.indirect(offs_sb[:, a // 16 : e // 16])
-            )
+        pair = keep.tile([P, T, 2], BF16, name="pair", align_bytes=64)
+        for c0, width, r in raw:
+            nc.vector.tensor_copy(out=pair[:, c0 : c0 + width, :], in_=r[:].rearrange("p j t -> p t j"))
+        nc.vector.tensor_copy(
+            out=words[:, 1, :], in_=pair[:].rearrange("p t j -> p (t j)").bitcast(U32).indirect(offs_sb[:])
+        )
+
+        plane1 = keep.tile([P, T], BF16, name="plane1", align_bytes=64)
+        c0 = 0
+        for width, act_cols in LAST_CHUNKS:
+            mid = c0 + width - act_cols
+            if mid > c0:
+                nc.gpsimd.tensor_scalar(
+                    out=plane1[:, c0:mid], in0=raw1[:, c0:mid], scalar1=1.0, scalar2=0.0, op0=ALU.mult, op1=ALU.add
+                )
+            nc.scalar.activation(plane1[:, mid : c0 + width], raw1[:, mid : c0 + width], ACT.Copy)
+            c0 += width
+        nc.vector.tensor_copy(out=grouped[:, :V_TOKENS, 1], in_=raw1[:].indirect(v_offs))
+        nc.scalar.activation(grouped[:, V_TOKENS:, 1], plane1[:].indirect(s_offs), ACT.Copy)
 
         x_codes = keep.tile([P, S], U32, name="x_codes", align_bytes=64)
         x_scales = keep.tile([P, S], U8, name="x_scales", align_bytes=64)
@@ -95,17 +114,13 @@ def tile_picked_sub_lin_gelu_sub_e_kernel(tc, xT, w, b, gate, offs, pos1, pos2, 
                 in_=grouped[:, a:e, :].rearrange("p s j -> p (s j)"),
             )
 
-        cast(0)
-        gather(0, 0, S)
-        cast(1)
-
         w_grouped = [keep.tile([P, P, 4], BF16, name=f"w_grouped{m}", align_bytes=64) for m in range(2)]
         w_codes = [keep.tile([P, P], U32, name=f"w_codes{m}", align_bytes=64) for m in range(2)]
         w_scales = [keep.tile([P, P], U8, name=f"w_scales{m}", align_bytes=64) for m in range(2)]
         for m in range(2):
             nc.gpsimd.tensor_scalar(
                 out=w_grouped[m][:],
-                in0=w_raw[:].rearrange("p j (c m) -> p m c j", m=2)[:, m, :, :],
+                in0=w_raw[m][:].rearrange("p j c -> p c j"),
                 scalar1=1.0,
                 scalar2=0.0,
                 op0=ALU.mult,
@@ -119,11 +134,9 @@ def tile_picked_sub_lin_gelu_sub_e_kernel(tc, xT, w, b, gate, offs, pos1, pos2, 
                 in_=w_grouped[m][:].rearrange("p n j -> p (n j)"),
             )
 
-        gather(1, 0, 768)
-        gather(1, 768, S)
         quantize_w(0)
-        for a in range(0, S, STEP):
-            quantize(a, a + STEP)
+        for a, e in SLICES:
+            quantize(a, e)
         quantize_w(1)
 
         y = [keep.tile([P, S], F32, name=f"y{m}") for m in range(2)]
@@ -141,10 +154,10 @@ def tile_picked_sub_lin_gelu_sub_e_kernel(tc, xT, w, b, gate, offs, pos1, pos2, 
             )
             nc.scalar.activation(y[m][:, a:e], bank[:], ACT.Gelu_apprx_tanh, bias=bias[:, m : m + 1])
 
-        for i in range(4):
-            layer(0, i * STEP, (i + 1) * STEP, f"bank{i}")
+        for i, (a, e) in enumerate(SLICES):
+            layer(0, a, e, f"bank{i}")
         for i in range(2):
-            layer(1, i * 512, (i + 1) * 512, f"bank{3 - i}")
+            layer(1, i * 512, (i + 1) * 512, f"bank{4 - i}")
 
         prod = [keep.tile([P, 2, V], F32, name=f"prod{d}") for d in range(D)]
         part = keep.tile([P, 2, V], F32, name="part")

@@ -18,9 +18,9 @@ ALU = mybir.AluOpType
 FLOPS = 2 * K * S * N
 
 PAIR_CHUNKS = (512, 512, 512, 256, 256)
-LAST_CHUNKS = ((1024, 384), (512, 256), (512, 512))
-V_TOKENS = 512
-SLICES = ((0, 256), (256, 512), (512, 768), (768, 896), (896, 1024))
+LAST_CHUNKS = ((1024, 384), (768, 256), (256, 256))
+V_TOKENS = 448
+SLICES = ((0, 256), (256, 512), (512, 768), (768, 1024))
 
 
 def tile_picked_sub_lin_gelu_sub_e_kernel(tc, xT, w, b, gate, offs, pos1, pos2, pos3, out):
@@ -59,10 +59,9 @@ def tile_picked_sub_lin_gelu_sub_e_kernel(tc, xT, w, b, gate, offs, pos1, pos2, 
         w_raw = [keep.tile([P, 4, P], F32, name=f"w_raw{m}") for m in range(2)]
         c0 = 0
         for width, act_cols in LAST_CHUNKS:
-            if c0 + width == T:
-                nc.sync.dma_start(out=w_raw[0][:], in_=w_view[:, :, :P])
             nc.sync.dma_start(out=raw1[:, c0 : c0 + width], in_=x_view[:, 1, c0 : c0 + width])
             c0 += width
+        nc.sync.dma_start(out=w_raw[0][:], in_=w_view[:, :, :P])
         nc.sync.dma_start(out=w_raw[1][:], in_=w_view[:, :, P:])
         bias = keep.tile([P, 2], F32, name="bias")
         nc.sync.dma_start(out=bias[:], in_=b.rearrange("(m p) o -> p (m o)", m=2))
@@ -157,19 +156,14 @@ def tile_picked_sub_lin_gelu_sub_e_kernel(tc, xT, w, b, gate, offs, pos1, pos2, 
         for i, (a, e) in enumerate(SLICES):
             layer(0, a, e, f"bank{i}")
         for i in range(2):
-            layer(1, i * 512, (i + 1) * 512, f"bank{4 - i}")
+            layer(1, i * 512, (i + 1) * 512, f"bank{3 - i}")
 
         prod = [keep.tile([P, 2, V], F32, name=f"prod{d}") for d in range(D)]
         part = keep.tile([P, 2, V], F32, name="part")
         res = keep.tile([P, 2, V], F32, name="res")
 
-        def neighbour(m, d, a=0, e=V):
-            nc.vector.tensor_tensor(
-                prod[d][:, m, a:e],
-                y[m][:].indirect(pos_sb[d][:, a // 16 : e // 16]),
-                gates[d][:, m, a:e],
-                ALU.mult,
-            )
+        def neighbour(m, d):
+            nc.vector.tensor_tensor(prod[d][:, m, :], y[m][:].indirect(pos_sb[d][:]), gates[d][:, m, :], ALU.mult)
 
         def last_sum(m, a=0, e=V):
             nc.vector.tensor_tensor(res[:, m, a:e], part[:, m, a:e], prod[2][:, m, a:e], ALU.add)
@@ -180,14 +174,13 @@ def tile_picked_sub_lin_gelu_sub_e_kernel(tc, xT, w, b, gate, offs, pos1, pos2, 
         neighbour(0, 2)
         neighbour(1, 0)
         neighbour(1, 1)
-        neighbour(1, 2, 0, 256)
+        neighbour(1, 2)
         nc.vector.tensor_tensor(
             part[:].rearrange("p m v -> p (m v)"),
             prod[0][:].rearrange("p m v -> p (m v)"),
             prod[1][:].rearrange("p m v -> p (m v)"),
             ALU.add,
         )
-        neighbour(1, 2, 256, V)
         last_sum(0)
-        last_sum(1, 0, 256)
-        last_sum(1, 256, V)
+        last_sum(1, 0, 384)
+        last_sum(1, 384, V)

from contextlib import ExitStack

import concourse.mybir as mybir

K, T, D, S, V, N = 512, 2048, 3, 1024, 512, 256
P = 128

F32 = mybir.dt.float32
BF16 = mybir.dt.bfloat16
U32 = mybir.dt.uint32
U16 = mybir.dt.uint16
U8 = mybir.dt.uint8
FP8X4 = mybir.dt.float8_e4m3fn_x4

ACT = mybir.ActivationFunctionType
ALU = mybir.AluOpType

FLOPS = 2 * K * S * N

PAIR_CHUNKS = (512, 512, 512, 256, 256)
LAST_CHUNKS = ((1024, 384), (768, 256), (256, 256))
V_TOKENS = 448
SLICES = ((0, 256), (256, 512), (512, 768), (768, 1024))


def tile_picked_sub_lin_gelu_sub_e_kernel(tc, xT, w, b, gate, offs, pos1, pos2, pos3, out):
    nc = tc.nc
    x_view = xT.rearrange("(p j) t -> p j t", j=4)
    gate_view = gate.rearrange("d (m p) v -> d p m v", m=2)
    out_view = out.rearrange("(m p) v -> p m v", m=2)

    with ExitStack() as ctx:
        lists = ctx.enter_context(tc.tile_pool(name="lists", bufs=1))
        keep = ctx.enter_context(tc.tile_pool(name="keep", bufs=1))
        psum = ctx.enter_context(tc.psum_pool(name="psum", bufs=1))

        offs_sb = lists.tile([P, S // 16], U16, name="offs_sb")
        pos_sb = [lists.tile([P, V // 16], U16, name=f"pos_sb{d}") for d in range(D)]

        zero = keep.tile([P, 1], F32, name="zero")
        nc.vector.memset(zero[:], 0.0)
        warm = keep.tile([P, 1], F32, name="warm")
        nc.scalar.activation(warm[:], zero[:], ACT.Gelu_apprx_tanh)

        raw0 = keep.tile([P, T], F32, name="raw0")
        raw1 = keep.tile([P, T], F32, name="raw1")
        half = T // 2
        nc.sync.dma_start(out=raw0[:, :half], in_=x_view[:, 0, :half])
        nc.sync.dma_start(offs_sb[:], offs)
        nc.sync.dma_start(out=raw0[:, half:], in_=x_view[:, 0, half:])
        raw = []
        c0 = 0
        for i, width in enumerate(PAIR_CHUNKS):
            r = keep.tile([P, 2, width], F32, name=f"raw23_{i}")
            nc.sync.dma_start(out=r[:], in_=x_view[:, 2:4, c0 : c0 + width])
            raw.append((c0, width, r))
            c0 += width
        w_view = w.rearrange("(p j) c -> p j c", j=4)
        w_raw = [keep.tile([P, 4, P], F32, name=f"w_raw{m}") for m in range(2)]
        c0 = 0
        for width, act_cols in LAST_CHUNKS:
            nc.sync.dma_start(out=raw1[:, c0 : c0 + width], in_=x_view[:, 1, c0 : c0 + width])
            c0 += width
        nc.sync.dma_start(out=w_raw[0][:], in_=w_view[:, :, :P])
        nc.sync.dma_start(out=w_raw[1][:], in_=w_view[:, :, P:])
        bias = keep.tile([P, 2], F32, name="bias")
        nc.sync.dma_start(out=bias[:], in_=b.rearrange("(m p) o -> p (m o)", m=2))
        gates = []
        for d, p_in in enumerate((pos1, pos2, pos3)):
            nc.sync.dma_start(pos_sb[d][:], p_in)
            g = keep.tile([P, 2, V], F32, name=f"gate{d}")
            nc.sync.dma_start(out=g[:], in_=gate_view[d])
            gates.append(g)

        grouped = keep.tile([P, S, 4], BF16, name="grouped", align_bytes=64)
        words = grouped[:].rearrange("p s j -> p (s j)").bitcast(U32).rearrange("p (s u) -> p u s", u=2)
        v_offs = offs_sb[:, 0 : V_TOKENS // 16]
        s_offs = offs_sb[:, V_TOKENS // 16 : S // 16]

        plane0 = keep.tile([P, T], BF16, name="plane0", align_bytes=64)
        for a in (0, half):
            nc.scalar.activation(plane0[:, a : a + half], raw0[:, a : a + half], ACT.Copy)
        nc.vector.tensor_copy(out=grouped[:, :V_TOKENS, 0], in_=raw0[:].indirect(v_offs))
        nc.scalar.activation(grouped[:, V_TOKENS:, 0], plane0[:].indirect(s_offs), ACT.Copy)

        pair = keep.tile([P, T, 2], BF16, name="pair", align_bytes=64)
        for c0, width, r in raw:
            nc.vector.tensor_copy(out=pair[:, c0 : c0 + width, :], in_=r[:].rearrange("p j t -> p t j"))
        nc.vector.tensor_copy(
            out=words[:, 1, :], in_=pair[:].rearrange("p t j -> p (t j)").bitcast(U32).indirect(offs_sb[:])
        )

        plane1 = keep.tile([P, T], BF16, name="plane1", align_bytes=64)
        c0 = 0
        for width, act_cols in LAST_CHUNKS:
            mid = c0 + width - act_cols
            if mid > c0:
                nc.gpsimd.tensor_scalar(
                    out=plane1[:, c0:mid], in0=raw1[:, c0:mid], scalar1=1.0, scalar2=0.0, op0=ALU.mult, op1=ALU.add
                )
            nc.scalar.activation(plane1[:, mid : c0 + width], raw1[:, mid : c0 + width], ACT.Copy)
            c0 += width
        nc.vector.tensor_copy(out=grouped[:, :V_TOKENS, 1], in_=raw1[:].indirect(v_offs))
        nc.scalar.activation(grouped[:, V_TOKENS:, 1], plane1[:].indirect(s_offs), ACT.Copy)

        x_codes = keep.tile([P, S], U32, name="x_codes", align_bytes=64)
        x_scales = keep.tile([P, S], U8, name="x_scales", align_bytes=64)

        def quantize(a, e):
            nc.vector.quantize_mx(
                out=x_codes[:, a:e].bitcast(FP8X4),
                scales=x_scales[:, a:e],
                in_=grouped[:, a:e, :].rearrange("p s j -> p (s j)"),
            )

        w_grouped = [keep.tile([P, P, 4], BF16, name=f"w_grouped{m}", align_bytes=64) for m in range(2)]
        w_codes = [keep.tile([P, P], U32, name=f"w_codes{m}", align_bytes=64) for m in range(2)]
        w_scales = [keep.tile([P, P], U8, name=f"w_scales{m}", align_bytes=64) for m in range(2)]
        for m in range(2):
            nc.gpsimd.tensor_scalar(
                out=w_grouped[m][:],
                in0=w_raw[m][:].rearrange("p j c -> p c j"),
                scalar1=1.0,
                scalar2=0.0,
                op0=ALU.mult,
                op1=ALU.add,
            )

        def quantize_w(m):
            nc.vector.quantize_mx(
                out=w_codes[m][:].bitcast(FP8X4),
                scales=w_scales[m][:],
                in_=w_grouped[m][:].rearrange("p n j -> p (n j)"),
            )

        quantize_w(0)
        for a, e in SLICES:
            quantize(a, e)
        quantize_w(1)

        y = [keep.tile([P, S], F32, name=f"y{m}") for m in range(2)]

        def layer(m, a, e, tag):
            bank = psum.tile([P, e - a], F32, name=f"acc{m}_{a}", tag=tag)
            nc.tensor.matmul_mx(
                out=bank[:],
                lhsT=w_codes[m][:].bitcast(FP8X4),
                lhsT_scale=w_scales[m][:],
                rhs=x_codes[:, a:e].bitcast(FP8X4),
                rhs_scale=x_scales[:, a:e],
                start=True,
                stop=True,
            )
            nc.scalar.activation(y[m][:, a:e], bank[:], ACT.Gelu_apprx_tanh, bias=bias[:, m : m + 1])

        for i, (a, e) in enumerate(SLICES):
            layer(0, a, e, f"bank{i}")
        for i in range(2):
            layer(1, i * 512, (i + 1) * 512, f"bank{3 - i}")

        prod = [keep.tile([P, 2, V], F32, name=f"prod{d}") for d in range(D)]
        part = keep.tile([P, 2, V], F32, name="part")
        res = keep.tile([P, 2, V], F32, name="res")

        def neighbour(m, d):
            nc.vector.tensor_tensor(prod[d][:, m, :], y[m][:].indirect(pos_sb[d][:]), gates[d][:, m, :], ALU.mult)

        def last_sum(m, a=0, e=V):
            nc.vector.tensor_tensor(res[:, m, a:e], part[:, m, a:e], prod[2][:, m, a:e], ALU.add)
            nc.sync.dma_start(out=out_view[:, m, a:e], in_=res[:, m, a:e])

        neighbour(0, 0)
        neighbour(0, 1)
        neighbour(0, 2)
        neighbour(1, 0)
        neighbour(1, 1)
        neighbour(1, 2)
        nc.vector.tensor_tensor(
            part[:].rearrange("p m v -> p (m v)"),
            prod[0][:].rearrange("p m v -> p (m v)"),
            prod[1][:].rearrange("p m v -> p (m v)"),
            ALU.add,
        )
        last_sum(0)
        last_sum(1, 0, 384)
        last_sum(1, 384, V)
